import numpy as np
import ml_dtypes


def mxq(x, axis, fmt="e4m3"):
    dtype, down = {"e4m3": (ml_dtypes.float8_e4m3fn, 7), "e5m2": (ml_dtypes.float8_e5m2, 14)}[fmt]
    v = np.moveaxis(np.asarray(x, np.float32).astype(ml_dtypes.bfloat16).astype(np.float64), axis, -1)
    blocks = v.reshape(v.shape[:-1] + (-1, 32))
    amax = np.abs(blocks).max(-1, keepdims=True)
    byte = np.maximum(np.where(amax > 0, np.frexp(amax)[1] - 1 + 127, 0) - down, 1)
    scale = np.exp2(byte - 127.0)
    codes = (blocks / scale).astype(np.float32).astype(dtype).astype(np.float64)
    return np.moveaxis((codes * scale).reshape(v.shape), -1, axis)


WIDE = False


def mx_kscale(k):
    if not WIDE:
        return np.ones(k)
    levels = np.array([10, -10, 5, -5, 0])
    if k % 512:
        return np.exp2(np.random.permutation(np.resize(levels, k // 32))).repeat(32)
    a = np.empty((k // 512, 16))
    for p in range(k // 512):
        a[p, :8] = np.random.permutation(np.resize(levels, 8))
        for g in range(8):
            far = levels[np.abs(levels - a[p, g]) >= 10]
            a[p, g + 8] = far[np.random.randint(len(far))]
    return np.exp2(a.ravel()).repeat(32)


BF16 = ml_dtypes.bfloat16


def bf(x):
    return np.asarray(x, np.float32).astype(BF16)


def f64(x):
    return np.asarray(x).astype(np.float64)


E2M1 = np.array([0.0, 0.5, 1.0, 1.5, 2.0, 3.0, 4.0, 6.0, -0.0, -0.5, -1.0, -1.5, -2.0, -3.0, -4.0, -6.0])


def pack_weight(w, fmt):
    k, n = w.shape
    w = f64(bf(w)).reshape(k // 32, 32, n)
    amax = np.abs(w).max(1)
    if fmt == "e4m3":
        byte = np.frexp(amax)[1] - 1 + 127 - 7
    else:
        mant, ex = np.frexp(amax / 6.0)
        byte = np.where(mant > 0.5, ex, ex - 1) + 127
    byte = np.clip(np.where(amax > 0, byte, 1), 1, 254)
    scaled = (w * np.exp2(127.0 - byte)[:, None, :]).reshape(k, n).astype(np.float32)
    by_word = np.ascontiguousarray(scaled.reshape(k // 512, 128, 4, n).transpose(0, 1, 3, 2))
    if fmt == "e4m3":
        words = by_word.astype(ml_dtypes.float8_e4m3fn).view(np.uint8)
    else:
        c = by_word.astype(ml_dtypes.float4_e2m1fn).view(np.uint8) & 0xF
        words = c[..., 0::2] | (c[..., 1::2] << 4)
    return np.ascontiguousarray(words), np.ascontiguousarray(byte.astype(np.uint8).reshape(k // 512, 16, n))


def unpack_weight(words, scales, fmt):
    g, p, n, _ = words.shape
    if fmt == "e4m3":
        vals = np.ascontiguousarray(words).view(ml_dtypes.float8_e4m3fn).astype(np.float64)
    else:
        nib = np.empty((g, p, n, 4), np.uint8)
        nib[..., 0::2] = words & 0xF
        nib[..., 1::2] = words >> 4
        vals = E2M1[nib]
    vals = vals * np.repeat(np.exp2(scales.astype(np.float64) - 127.0), 8, axis=1)[..., None]
    return vals.transpose(0, 1, 3, 2).reshape(g * 512, n)
def pack4(w):
    words, scales = pack_weight(w, "e2m1")
    return words.reshape(words.shape[0], 128, -1), scales


def unpack4(words, scales):
    return unpack_weight(words.reshape(words.shape[0], 128, -1, 2), scales, "e2m1")


E4M3FN = np.array([(-1.0 if i & 128 else 1.0) * ((1.0 + (i & 7) / 8.0) * 2.0 ** (((i >> 3) & 15) - 7) if i & 120 else (i & 7) * 2.0 ** -9) for i in range(256)])


def e4m3fn_bytes(y):
    return np.clip(np.asarray(y, np.float64), -448.0, 448.0).astype(np.float32).astype(ml_dtypes.float8_e4m3fn).view(np.uint8)


def e4m3fn_values(b):
    return E4M3FN[b]


B, D, K = 1024, 512, 1024


def features(uq, wq, gain):
    return np.tanh(uq @ wq) * gain


def pair_kernel(a, b):
    return (mxq(a, 1, "e4m3") @ mxq(b, 1, "e4m3").T) / np.sqrt(a.shape[-1])


def draw0():
    s, t = mx_kscale(D), mx_kscale(K)
    x = bf(np.random.standard_normal((B, D)) * s)
    xn = bf(np.random.standard_normal((B, D)) * s)
    w_words, w_scales = pack4(np.random.standard_normal((D, K)) / np.sqrt(D) / s[:, None])
    wt_words, wt_scales = pack4(np.random.standard_normal((D, K)) / np.sqrt(D) / s[:, None])
    g1 = bf((1.0 + 0.1 * np.random.standard_normal(K)) * t)
    g2 = bf((1.0 + 0.1 * np.random.standard_normal(K)) / t)
    r = bf(np.random.uniform(0.0, 1.0, B))
    return {"x": x, "xn": xn, "w_words": w_words, "w_scales": w_scales, "wt_words": wt_words, "wt_scales": wt_scales, "g1": g1, "g2": g2, "r": r}


def core(x, xn, w_words, w_scales, wt_words, wt_scales, g1, g2, r):
    xq = mxq(f64(x), 1, "e4m3")
    xnq = mxq(f64(xn), 1, "e4m3")
    wq = unpack4(w_words, w_scales)
    wtq = unpack4(wt_words, wt_scales)
    g1, g2, r = f64(g1), f64(g2), f64(r)
    p = features(xq, wq, g1)
    q = features(xq, wtq, g2)
    pn = features(xnq, wq, g1)
    qn = features(xnq, wtq, g2)
    k0 = pair_kernel(p, q)
    k1 = pair_kernel(pn, qn)
    tgt = 1.0 - np.abs(r[:, None] - r[None, :]) + 0.9 * k1
    return k0 - tgt


def setup_inputs():
    drawn = draw0()
    full = np.asarray(drawn['xn']).astype(np.float64)
    scale = (np.abs(full).reshape(1024, 4, 128).max(axis=(2,)) / 448.0).astype(np.float32)
    given = {}
    for key, value in drawn.items():
        if key == 'xn':
            given['xn_bytes'] = e4m3fn_bytes(full / np.repeat(scale.astype(np.float64), 128, axis=1))
            given['xn_scale'] = scale
        else:
            given[key] = value
    return given


def reference(x, xn_bytes, xn_scale, w_words, w_scales, wt_words, wt_scales, g1, g2, r):
    return core(x, e4m3fn_values(xn_bytes) * np.repeat(xn_scale.astype(np.float64), 128, axis=1), w_words, w_scales, wt_words, wt_scales, g1, g2, r)

@@ -1,0 +1,369 @@
+from contextlib import ExitStack
+
+import concourse.mybir as mybir
+from concourse.masks import make_identity
+
+B, D, K = 1024, 512, 1024
+FLOPS = 4 * 2 * B * D * K + 2 * 2 * B * B * K
+
+F32 = mybir.dt.float32
+BF16 = mybir.dt.bfloat16
+I32 = mybir.dt.int32
+U32 = mybir.dt.uint32
+U8 = mybir.dt.uint8
+F8 = mybir.dt.float8_e4m3fn
+FP8X4 = mybir.dt.float8_e4m3fn_x4
+FP4X4 = mybir.dt.float4_e2m1fn_x4
+ALU = mybir.AluOpType
+ACT = mybir.ActivationFunctionType
+
+P = 128
+RATE = lambda step: RATES[step // 4]
+XQ_AT = {0: ((0, 2),), 1: ((0, 3),), 7: ((1, 0), (1, 1)), 12: ((1, 2), (1, 3))}
+TURN_AT = {1: ((0, 2),), 2: ((0, 3),), 7: ((1, 0),), 8: ((1, 1),), 11: ((1, 2),), 13: ((1, 3),)}
+EVAC = lambda nc, which, c: nc.vector.tensor_copy if which == 0 else nc.scalar.copy
+WIDEN_SCALAR = range(8)
+ON_GPSIMD = frozenset((3, 4, 6, 10, 11, 13, 15, 17, 18, 20, 21, 25, 26, 29, ))
+FLUSH = frozenset((0, 3, 4, 5, 6, 7, 8, 9, 10, 11, 12, 13, 14, 16, 17, 19, 20, 22, 23, 24, 27, 28, 29, 30, ))
+DIST_AT = {3: (1,), 5: (2,), 10: (3,), 15: (4,), 18: (5,), 7: (6,), 19: (7,)}
+WIDEN_AT = {3: (0,), 4: (1, 3), 7: (2, 7), 8: (4,), 6: (5,), 10: (6,)}
+RATES = [2, 2, 2, 3, 2, 3, 3, 3]
+LEAD = 3
+GP_BUFS = 3
+
+
+def tile_kernelbehaviouralmetrictdresidual_d1p_kernel(
+    tc, x, xn_bytes, xn_scale, w_words, w_scales, wt_words, wt_scales, g1, g2, r, out
+):
+    nc = tc.nc
+    with ExitStack() as ctx:
+        ctx.enter_context(tc.manual_schedule())
+        keep = ctx.enter_context(tc.tile_pool(name="keep", bufs=1))
+        work = ctx.enter_context(tc.tile_pool(name="work", bufs=4))
+        psum = ctx.enter_context(tc.psum_pool(name="psum", bufs=1))
+
+        x_sb = keep.tile([P, 8, D], BF16, name="x_sb")
+        xb_sb = keep.tile([P, 8, D], U8, name="xb_sb")
+        xs_sb = keep.tile([P, 8, 4], F32, name="xs_sb")
+        xw_sb = keep.tile([P, 8, D], BF16, name="xw_sb")
+        x_codes = [keep.tile([P, B], U32, name="x_codes%d" % i, align_bytes=64) for i in range(2)]
+        x_scales = [keep.tile([P, B], U8, name="x_scales%d" % i, align_bytes=64) for i in range(2)]
+        raw_w = [keep.tile([P, 2 * K], U8, name="raw_w%d" % i, align_bytes=64) for i in range(2)]
+        raw_s = [keep.tile([P, K], U8, name="raw_s%d" % i, align_bytes=64) for i in range(2)]
+        perm_w = [keep.tile([P, 2 * K], U8, name="perm_w%d" % i, align_bytes=64) for i in range(2)]
+        perm_s = [keep.tile([P, K], U8, name="perm_s%d" % i, align_bytes=64) for i in range(2)]
+        f_codes = {}
+        f_scales = {}
+        for prod in ("q", "p", "qn", "pn"):
+            f_codes[prod] = keep.tile([P, 2, B], U32, name="codes_%s" % prod, align_bytes=64)
+            f_scales[prod] = keep.tile([P, 2, B], U8, name="scales_%s" % prod, align_bytes=64)
+        e_sb = keep.tile([P, 8, B], F32, name="e_sb")
+        ident_f = keep.tile([P, P], F32, name="ident_f")
+        ident_b = keep.tile([P, P], BF16, name="ident_b")
+        sel_g = keep.tile([P, 8], BF16, name="sel_g")
+        rows_r = keep.tile([P, 256], BF16, name="rows_r")
+        rows_g = keep.tile([P, 256], BF16, name="rows_g")
+        r_col = keep.tile([P, 8], F32, name="r_col")
+        g_col = keep.tile([P, 16], F32, name="g_col")
+        r_row = keep.tile([P, B], BF16, name="r_row")
+        warm = keep.tile([P, 1], F32, name="warm")
+        cols_ps = psum.tile([P, 24], F32, name="cols_ps", tag="cols", bufs=1)
+
+        x_v = x.rearrange("(n p) k -> p n k", p=P)
+
+        def load_x(c):
+            nc.sync.dma_start(out=x_sb[:, 2 * c : 2 * c + 2, :], in_=x_v[:, 2 * c : 2 * c + 2, :])
+
+        def load_words(i, src):
+            nc.sync.dma_start(out=raw_w[i][:].bitcast(I32), in_=src[0].bitcast(I32))
+
+        def load_scales(eng, i, src):
+            for quad in range(4):
+                eng.dma_start(
+                    out=raw_s[i][32 * quad : 32 * quad + 4, :].bitcast(I32),
+                    in_=src[0, 4 * quad : 4 * quad + 4, :].bitcast(I32),
+                )
+
+        nc.vector.memset(rows_r[:], 0.0)
+        nc.vector.memset(raw_s[0][:].bitcast(I32), 0)
+        nc.vector.memset(rows_g[:], 0.0)
+        nc.vector.memset(raw_s[1][:].bitcast(I32), 0)
+        nc.vector.memset(warm[:], 0.0)
+        make_identity(nc, ident_f[:])
+
+        load_x(0)
+        nc.scalar.dma_start(out=rows_r[0:4, :], in_=r.rearrange("(q n) -> q n", q=4))
+        load_words(0, wt_words)
+        load_scales(nc.scalar, 0, wt_scales)
+        load_x(1)
+        nc.gpsimd.dma_start(
+            out=rows_g[0:4, :].rearrange("t (m b) -> t m b", b=8), in_=g2.rearrange("(m t b) -> t m b", t=4, b=8)
+        )
+        nc.gpsimd.dma_start(
+            out=rows_g[4:8, :].rearrange("t (m b) -> t m b", b=8), in_=g1.rearrange("(m t b) -> t m b", t=4, b=8)
+        )
+        load_x(2)
+        load_words(1, w_words)
+        load_scales(nc.sync, 1, w_scales)
+        load_x(3)
+        nc.sync.dma_start(out=xs_sb[:], in_=xn_scale.rearrange("(n p) j -> p n j", p=P))
+        xb_v = xn_bytes.rearrange("(n p) k -> p n k", p=P)
+        for half in range(2):
+            nc.sync.dma_start(out=xb_sb[:, 4 * half : 4 * half + 4, :], in_=xb_v[:, 4 * half : 4 * half + 4, :])
+
+        nc.scalar.activation(out=warm[:], in_=warm[:], func=ACT.Tanh)
+
+        nc.vector.tensor_copy(out=ident_b[:], in_=ident_f[:])
+        nc.vector.tensor_scalar(out=sel_g[:, 0:4], in0=ident_f[:, 0:4], scalar1=1.0 / 32.0, scalar2=None, op0=ALU.mult)
+        nc.vector.tensor_copy(out=sel_g[:, 4:8], in_=ident_f[:, 4:8])
+
+        def permute_words(eng, i, g):
+            eng.tensor_copy(
+                out=perm_w[i][:].bitcast(I32)[:, 256 * g : 256 * g + 256].rearrange("p (t a b) -> p t a b", t=4, b=4),
+                in_=raw_w[i][:].bitcast(I32)[:, 256 * g : 256 * g + 256].rearrange("p (a t b) -> p t a b", t=4, b=4),
+            )
+
+        def permute_scales(eng, i, g):
+            eng.tensor_copy(
+                out=perm_s[i][:].bitcast(I32)[:, 128 * g : 128 * g + 128].rearrange("p (t a b) -> p t a b", t=4, b=2),
+                in_=raw_s[i][:].bitcast(I32)[:, 128 * g : 128 * g + 128].rearrange("p (a t b) -> p t a b", t=4, b=2),
+            )
+
+        def r_stage():
+            for h in range(2):
+                nc.tensor.matmul(
+                    out=cols_ps[:, 4 * h : 4 * h + 4], lhsT=rows_r[:, P * h : P * h + P], rhs=ident_b[:, 0:4], start=True, stop=True
+                )
+            for jh in range(2):
+                bank = psum.tile([P, 512], F32, name="bank_r", tag="kk", bufs=4)
+                for q in range(2):
+                    nc.tensor.matmul(
+                        out=bank[:, 256 * q : 256 * q + 256],
+                        lhsT=ident_b[:, 2 * jh + q : 2 * jh + q + 1].to_broadcast([P, P]),
+                        rhs=rows_r[:, :],
+                        start=True,
+                        stop=True,
+                    )
+                nc.vector.tensor_copy(out=r_row[:, 512 * jh : 512 * jh + 512], in_=bank[:])
+            nc.vector.tensor_copy(out=r_col[:], in_=cols_ps[:, 0:8])
+
+        def g_stage():
+            for h in range(2):
+                nc.tensor.matmul(
+                    out=cols_ps[:, 8 + 8 * h : 16 + 8 * h], lhsT=rows_g[:, P * h : P * h + P], rhs=sel_g[:, :], start=True, stop=True
+                )
+            nc.vector.tensor_copy(out=g_col[:], in_=cols_ps[:, 8:24])
+
+        def distance(i):
+            c = 4 * (i % 2) + i // 2
+            nc.scalar.activation(out=e_sb[:, i, :], in_=r_row[:], func=ACT.Abs, bias=r_col[:, c : c + 1], scale=-1.0)
+
+        def turn(src, c):
+            bank = psum.tile([P, 2, 2, P], F32, name="bank_t", tag="kk", bufs=4)
+            for a in range(2):
+                words = src[:, 2 * c + a, :].bitcast(F32)
+                for u in range(2):
+                    nc.tensor.transpose(bank[:, a, u, :], words[:, u:256:2], ident_f[:])
+            return bank
+
+        def unload(eng_copy, bank):
+            grouped = work.tile([P, 256, 4], BF16, name="grouped", tag="grouped", bufs=3, align_bytes=64)
+            eng_copy(
+                out=grouped[:].rearrange("p n t -> p (n t)").bitcast(F32).rearrange("p (a n u) -> p a n u", a=2, u=2),
+                in_=bank[:].rearrange("p a u n -> p a n u"),
+            )
+            return grouped
+
+        def quantise_x(which, c, grouped):
+            cols = slice(256 * c, 256 * c + 256)
+            nc.vector.quantize_mx(
+                out=x_codes[which][:, cols].bitcast(FP8X4),
+                scales=x_scales[which][:, cols],
+                in_=grouped[:].rearrange("p n t -> p (n t)"),
+            )
+
+        def widen(n, on_scalar):
+            for j in range(4):
+                src = xb_sb[:, n, P * j : P * j + P].bitcast(F8)
+                dst = xw_sb[:, n, P * j : P * j + P]
+                if on_scalar:
+                    nc.scalar.activation(out=dst, in_=src, func=ACT.Copy, scale=xs_sb[:, n, j : j + 1])
+                else:
+                    nc.vector.tensor_scalar(out=dst, in0=src, scalar1=xs_sb[:, n, j : j + 1], scalar2=None, op0=ALU.mult)
+
+        weight_of = {"q": 0, "qn": 0, "p": 1, "pn": 1}
+        x_of = {"q": 0, "p": 0, "qn": 1, "pn": 1}
+
+        def features(prod, units):
+            th = work.tile([P, 2, P, 4], F32, name="th", tag="th", bufs=8)
+            wi, xi = weight_of[prod], x_of[prod]
+            for u, (g, c) in enumerate(units):
+                bank = psum.tile([P, 4, P], F32, name="bank_f", tag="mm", bufs=3)
+                toks = slice(P * c, P * c + P)
+                for t in range(4):
+                    s = 4 * g + t
+                    nc.tensor.matmul_mx(
+                        out=bank[:, t, :],
+                        lhsT=perm_w[wi][:, 256 * s : 256 * s + 256].bitcast(FP4X4),
+                        lhsT_scale=perm_s[wi][:, P * s : P * s + P],
+                        rhs=x_codes[xi][:, toks].bitcast(FP8X4),
+                        rhs_scale=x_scales[xi][:, toks],
+                        start=True,
+                        stop=True,
+                    )
+                nc.scalar.activation(out=th[:, u, :, :], in_=bank[:].rearrange("p t n -> p n t"), func=ACT.Tanh)
+            return th
+
+        def gain(on_gpsimd, prod, units, th):
+            eng, gains = (nc.gpsimd, g_col[:]) if on_gpsimd else (nc.vector, cols_ps[:, 8:24])
+            c0 = 0 if weight_of[prod] == 0 else 4
+            if on_gpsimd:
+                scaled = work.tile([P, 2, P, 4], BF16, name="scaled_g", tag="scaled_g", bufs=GP_BUFS, align_bytes=64)
+            else:
+                scaled = work.tile([P, 2, P, 4], BF16, name="scaled", tag="scaled", bufs=5, align_bytes=64)
+            if units[0][0] == units[1][0]:
+                c0 += 8 * units[0][0]
+                eng.tensor_tensor(
+                    out=scaled[:].rearrange("p u n t -> p (u n) t"),
+                    in0=th[:].rearrange("p u n t -> p (u n) t"),
+                    in1=gains[:, c0 : c0 + 4].unsqueeze(1).to_broadcast([P, 256, 4]),
+                    op=ALU.mult,
+                )
+            else:
+                eng.tensor_tensor(
+                    out=scaled[:],
+                    in0=th[:],
+                    in1=gains.rearrange("p (g c) -> p g c", g=2)[:, :, c0 : c0 + 4].unsqueeze(2).to_broadcast([P, 2, P, 4]),
+                    op=ALU.mult,
+                )
+            return scaled
+
+        def quantise_f(prod, units, scaled):
+            if units[0][0] == units[1][0]:
+                runs = [(units[0], 256, scaled[:])]
+            else:
+                runs = [(units[u], P, scaled[:, u : u + 1, :, :]) for u in range(2)]
+            for (g, c), width, src in runs:
+                cols = slice(P * c, P * c + width)
+                nc.vector.quantize_mx(
+                    out=f_codes[prod][:, g, cols].bitcast(FP8X4),
+                    scales=f_scales[prod][:, g, cols],
+                    in_=src.rearrange("p u n t -> p (u n t)"),
+                )
+
+        def pair(i, jh, nxt):
+            a, b = ("pn", "qn") if nxt else ("p", "q")
+            bank = psum.tile([P, 512], F32, name="bank_k", tag="kk", bufs=4)
+            rows = slice(P * i, P * i + P)
+            cols = slice(512 * jh, 512 * jh + 512)
+            for g in range(2):
+                nc.tensor.matmul_mx(
+                    out=bank[:],
+                    lhsT=f_codes[a][:, g, rows].bitcast(FP8X4),
+                    lhsT_scale=f_scales[a][:, g, rows],
+                    rhs=f_codes[b][:, g, cols].bitcast(FP8X4),
+                    rhs_scale=f_scales[b][:, g, cols],
+                    start=(g == 0),
+                    stop=(g == 1),
+                )
+            return bank
+
+        def finish(i, jh, nxt, bank):
+            rows = slice(P * i, P * i + P)
+            cols = slice(512 * jh, 512 * jh + 512)
+            e = e_sb[:, i, cols]
+            if nxt:
+                res = work.tile([P, 512], F32, name="res", tag="res", bufs=6)
+                nc.vector.scalar_tensor_tensor(out=res[:], in0=bank[:], scalar=-0.9, in1=e, op0=ALU.mult, op1=ALU.add)
+                nc.sync.dma_start(out=out[rows, cols], in_=res[:])
+            else:
+                nc.vector.scalar_tensor_tensor(out=e, in0=bank[:], scalar=-1.0, in1=e, op0=ALU.add, op1=ALU.add)
+
+        r_stage()
+        bank_t = turn(x_sb, 0)
+        permute_words(nc.vector, 0, 0)
+        permute_scales(nc.vector, 0, 0)
+        grouped = unload(nc.vector.tensor_copy, bank_t)
+        bank_t = turn(x_sb, 1)
+        distance(0)
+        quantise_x(0, 0, grouped)
+        grouped = unload(nc.scalar.copy, bank_t)
+        permute_words(nc.vector, 0, 1)
+        permute_scales(nc.vector, 0, 1)
+        g_stage()
+        quantise_x(0, 1, grouped)
+        for g in range(2):
+            permute_words(nc.vector, 1, g)
+            permute_scales(nc.vector, 1, g)
+
+        order = []
+        for a, b in (("q", "p"), ("qn", "pn")):
+            for prod, c in ((a, 0), (a, 1), (b, 0), (b, 1), (a, 2), (a, 3), (b, 2), (b, 3)):
+                if prod == "pn" and c == 3:
+                    order.extend([(prod, ((0, 6), (1, 6))), (prod, ((0, 7), (1, 7)))])
+                else:
+                    order.extend([(prod, ((g, 2 * c), (g, 2 * c + 1))) for g in range(2)])
+
+        have = set()
+        waiting = []
+        for nxt in (0, 1):
+            for jh in range(2):
+                waiting.extend([(i, jh, nxt) for i in range(8)])
+
+        def ready_tiles():
+            found = []
+            for i, jh, nxt in waiting:
+                a, b = ("pn", "qn") if nxt else ("p", "q")
+                need = set([(a, g, i) for g in range(2)] + [(b, g, 4 * jh + m) for g in range(2) for m in range(4)])
+                if need <= have:
+                    found.append((i, jh, nxt))
+            for key in found:
+                waiting.remove(key)
+            return found
+
+        ready = []
+        banks = []
+        due = []
+        ths = []
+        grouped_of = {}
+
+        def first_stage(step):
+            if step < len(order):
+                ths.append(features(*order[step]))
+            for i in DIST_AT.get(step, ()):
+                distance(i)
+            for n in WIDEN_AT.get(step, ()):
+                widen(n, n in WIDEN_SCALAR)
+            for which, c in TURN_AT.get(step, ()):
+                bank = turn((x_sb, xw_sb)[which], c)
+                grouped_of[(which, c)] = unload(EVAC(nc, which, c), bank)
+
+        def flush():
+            for flag in (False, True):
+                for item in due:
+                    if item[0] == flag:
+                        quantise_f(*item[1:])
+                        have.update([(item[1], g, c) for g, c in item[2]])
+            due.clear()
+
+        for step in range(LEAD):
+            first_stage(step)
+        for step, (prod, units) in enumerate(order):
+            first_stage(step + LEAD)
+            on_gp = step in ON_GPSIMD
+            scaled = gain(on_gp, prod, units, ths[step])
+            for key in XQ_AT.get(step, ()):
+                quantise_x(*key, grouped_of[key])
+            if step in FLUSH:
+                flush()
+            due.append((on_gp, prod, units, scaled))
+            for key, bank in banks:
+                finish(*key, bank)
+            rate = RATE(step)
+            banks = [(key, pair(*key)) for key in ready[:rate]]
+            ready = ready[rate:] + ready_tiles()
+        flush()
+        for key, bank in banks:
+            finish(*key, bank)
+        for key in ready + ready_tiles():
+            finish(*key, pair(*key))

@@ -19,17 +19,19 @@ ACT = mybir.ActivationFunctionType
 
 P = 128
 RATE = lambda step: RATES[step // 4]
-XQ_AT = {0: ((0, 2),), 1: ((0, 3),), 7: ((1, 0), (1, 1)), 12: ((1, 2), (1, 3))}
-TURN_AT = {1: ((0, 2),), 2: ((0, 3),), 7: ((1, 0),), 8: ((1, 1),), 11: ((1, 2),), 13: ((1, 3),)}
-EVAC = lambda nc, which, c: nc.vector.tensor_copy if which == 0 else nc.scalar.copy
-WIDEN_SCALAR = range(8)
-ON_GPSIMD = frozenset((3, 4, 6, 10, 11, 13, 15, 17, 18, 20, 21, 25, 26, 29, ))
-FLUSH = frozenset((0, 3, 4, 5, 6, 7, 8, 9, 10, 11, 12, 13, 14, 16, 17, 19, 20, 22, 23, 24, 27, 28, 29, 30, ))
-DIST_AT = {3: (1,), 5: (2,), 10: (3,), 15: (4,), 18: (5,), 7: (6,), 19: (7,)}
-WIDEN_AT = {3: (0,), 4: (1, 3), 7: (2, 7), 8: (4,), 6: (5,), 10: (6,)}
-RATES = [2, 2, 2, 3, 2, 3, 3, 3]
-LEAD = 3
-GP_BUFS = 3
+XQ_AT = {1: ((0, 2),), 3: ((0, 3),), 8: ((1, 0),), 10: ((1, 1),), 13: ((1, 2),), 16: ((1, 3),)}
+TURN_AT = {2: ((0, 2),), 3: ((0, 3),), 8: ((1, 0),), 10: ((1, 1),), 12: ((1, 2),), 15: ((1, 3),)}
+EVAC = lambda nc, which, c: nc.scalar.copy
+WIDEN_SCALAR = ()
+W_AT = 1
+R_AT = 3
+ON_GPSIMD = frozenset()
+FLUSH = frozenset((0, 1, 2, 3, 4, 5, 6, 7, 8, 9, 10, 11, 12, 13, 14, 15, 16, 17, 18, 19, 20, 21, 22, 23, 24, 25, 26, 27, 28, 29, 30, 31, ))
+DIST_AT = {4: (0,), 6: (1,), 7: (2,), 9: (3,), 14: (4,), 16: (5,), 17: (6,), 18: (7,)}
+WIDEN_AT = {3: (0, 1), 5: (2, 3), 9: (4, 5), 10: (6, 7)}
+RATES = [1, 1, 1, 1, 2, 2, 2, 2]
+LEAD = 2
+GP_BUFS = 2
 
 
 def tile_kernelbehaviouralmetrictdresidual_d1p_kernel(
@@ -60,9 +62,9 @@ def tile_kernelbehaviouralmetrictdresidual_d1p_kernel(
         e_sb = keep.tile([P, 8, B], F32, name="e_sb")
         ident_f = keep.tile([P, P], F32, name="ident_f")
         ident_b = keep.tile([P, P], BF16, name="ident_b")
-        sel_g = keep.tile([P, 8], BF16, name="sel_g")
+        sel_g = keep.tile([P, 4], BF16, name="sel_g")
         rows_r = keep.tile([P, 256], BF16, name="rows_r")
-        rows_g = keep.tile([P, 256], BF16, name="rows_g")
+        rows_g = [keep.tile([P, 256], BF16, name="rows_g%d" % i) for i in range(2)]
         r_col = keep.tile([P, 8], F32, name="r_col")
         g_col = keep.tile([P, 16], F32, name="g_col")
         r_row = keep.tile([P, B], BF16, name="r_row")
@@ -70,9 +72,6 @@ def tile_kernelbehaviouralmetrictdresidual_d1p_kernel(
         cols_ps = psum.tile([P, 24], F32, name="cols_ps", tag="cols", bufs=1)
 
         x_v = x.rearrange("(n p) k -> p n k", p=P)
-
-        def load_x(c):
-            nc.sync.dma_start(out=x_sb[:, 2 * c : 2 * c + 2, :], in_=x_v[:, 2 * c : 2 * c + 2, :])
 
         def load_words(i, src):
             nc.sync.dma_start(out=raw_w[i][:].bitcast(I32), in_=src[0].bitcast(I32))
@@ -84,28 +83,26 @@ def tile_kernelbehaviouralmetrictdresidual_d1p_kernel(
                     in_=src[0, 4 * quad : 4 * quad + 4, :].bitcast(I32),
                 )
 
-        nc.vector.memset(rows_r[:], 0.0)
         nc.vector.memset(raw_s[0][:].bitcast(I32), 0)
-        nc.vector.memset(rows_g[:], 0.0)
+        nc.vector.memset(rows_r[:], 0.0)
+        nc.vector.memset(rows_g[0][:], 0.0)
+        nc.vector.memset(rows_g[1][:], 0.0)
         nc.vector.memset(raw_s[1][:].bitcast(I32), 0)
         nc.vector.memset(warm[:], 0.0)
         make_identity(nc, ident_f[:])
 
-        load_x(0)
-        nc.scalar.dma_start(out=rows_r[0:4, :], in_=r.rearrange("(q n) -> q n", q=4))
+        nc.sync.dma_start(out=x_sb[:, 0, :], in_=x_v[:, 0, :])
         load_words(0, wt_words)
         load_scales(nc.scalar, 0, wt_scales)
-        load_x(1)
-        nc.gpsimd.dma_start(
-            out=rows_g[0:4, :].rearrange("t (m b) -> t m b", b=8), in_=g2.rearrange("(m t b) -> t m b", t=4, b=8)
-        )
-        nc.gpsimd.dma_start(
-            out=rows_g[4:8, :].rearrange("t (m b) -> t m b", b=8), in_=g1.rearrange("(m t b) -> t m b", t=4, b=8)
-        )
-        load_x(2)
+        nc.sync.dma_start(out=x_sb[:, 1:4, :], in_=x_v[:, 1:4, :])
+        nc.sync.dma_start(out=x_sb[:, 4:8, :], in_=x_v[:, 4:8, :])
+        for src, dst in ((g2, rows_g[0]), (g1, rows_g[1])):
+            nc.gpsimd.dma_start(
+                out=dst[0:4, :].rearrange("t (m b) -> t m b", b=8), in_=src.rearrange("(m t b) -> t m b", t=4, b=8)
+            )
+        nc.gpsimd.dma_start(out=rows_r[0:4, :], in_=r.rearrange("(q n) -> q n", q=4))
         load_words(1, w_words)
         load_scales(nc.sync, 1, w_scales)
-        load_x(3)
         nc.sync.dma_start(out=xs_sb[:], in_=xn_scale.rearrange("(n p) j -> p n j", p=P))
         xb_v = xn_bytes.rearrange("(n p) k -> p n k", p=P)
         for half in range(2):
@@ -114,8 +111,7 @@ def tile_kernelbehaviouralmetrictdresidual_d1p_kernel(
         nc.scalar.activation(out=warm[:], in_=warm[:], func=ACT.Tanh)
 
         nc.vector.tensor_copy(out=ident_b[:], in_=ident_f[:])
-        nc.vector.tensor_scalar(out=sel_g[:, 0:4], in0=ident_f[:, 0:4], scalar1=1.0 / 32.0, scalar2=None, op0=ALU.mult)
-        nc.vector.tensor_copy(out=sel_g[:, 4:8], in_=ident_f[:, 4:8])
+        nc.vector.tensor_scalar(out=sel_g[:], in0=ident_f[:, 0:4], scalar1=1.0 / 32.0, scalar2=None, op0=ALU.mult)
 
         def permute_words(eng, i, g):
             eng.tensor_copy(
@@ -128,6 +124,8 @@ def tile_kernelbehaviouralmetrictdresidual_d1p_kernel(
                 out=perm_s[i][:].bitcast(I32)[:, 128 * g : 128 * g + 128].rearrange("p (t a b) -> p t a b", t=4, b=2),
                 in_=raw_s[i][:].bitcast(I32)[:, 128 * g : 128 * g + 128].rearrange("p (a t b) -> p t a b", t=4, b=2),
             )
+
+        r_banks = []
 
         def r_stage():
             for h in range(2):
@@ -144,15 +142,24 @@ def tile_kernelbehaviouralmetrictdresidual_d1p_kernel(
                         start=True,
                         stop=True,
                     )
-                nc.vector.tensor_copy(out=r_row[:, 512 * jh : 512 * jh + 512], in_=bank[:])
-            nc.vector.tensor_copy(out=r_col[:], in_=cols_ps[:, 0:8])
+                r_banks.append(bank)
 
-        def g_stage():
+        def r_copies():
+            for jh in range(2):
+                nc.scalar.copy(out=r_row[:, 512 * jh : 512 * jh + 512], in_=r_banks[jh][:])
+            nc.scalar.copy(out=r_col[:], in_=cols_ps[:, 0:8])
+
+        def g_stage(side):
             for h in range(2):
                 nc.tensor.matmul(
-                    out=cols_ps[:, 8 + 8 * h : 16 + 8 * h], lhsT=rows_g[:, P * h : P * h + P], rhs=sel_g[:, :], start=True, stop=True
+                    out=cols_ps[:, 8 + 8 * h + 4 * side : 12 + 8 * h + 4 * side],
+                    lhsT=rows_g[side][:, P * h : P * h + P],
+                    rhs=(sel_g, ident_b)[side][:, 0:4],
+                    start=True,
+                    stop=True,
                 )
-            nc.vector.tensor_copy(out=g_col[:], in_=cols_ps[:, 8:24])
+            if ON_GPSIMD and side == 1:
+                nc.vector.tensor_copy(out=g_col[:], in_=cols_ps[:, 8:24])
 
         def distance(i):
             c = 4 * (i % 2) + i // 2
@@ -173,6 +180,29 @@ def tile_kernelbehaviouralmetrictdresidual_d1p_kernel(
                 in_=bank[:].rearrange("p a u n -> p a n u"),
             )
             return grouped
+
+        def turn_one(n):
+            bank = psum.tile([P, 2, P], F32, name="bank_t1", tag="mm", bufs=3)
+            words = x_sb[:, n, :].bitcast(F32)
+            for u in range(2):
+                nc.tensor.transpose(bank[:, u, :], words[:, u:256:2], ident_f[:])
+            return bank
+
+        def unload_one(eng_copy, bank):
+            grouped = work.tile([P, P, 4], BF16, name="grouped1", tag="grouped1", bufs=2, align_bytes=64)
+            eng_copy(
+                out=grouped[:].rearrange("p n t -> p (n t)").bitcast(F32).rearrange("p (n u) -> p n u", u=2),
+                in_=bank[:].rearrange("p u n -> p n u"),
+            )
+            return grouped
+
+        def quantise_one(n, grouped):
+            cols = slice(P * n, P * n + P)
+            nc.vector.quantize_mx(
+                out=x_codes[0][:, cols].bitcast(FP8X4),
+                scales=x_scales[0][:, cols],
+                in_=grouped[:].rearrange("p n t -> p (n t)"),
+            )
 
         def quantise_x(which, c, grouped):
             cols = slice(256 * c, 256 * c + 256)
@@ -214,14 +244,23 @@ def tile_kernelbehaviouralmetrictdresidual_d1p_kernel(
                 nc.scalar.activation(out=th[:, u, :, :], in_=bank[:].rearrange("p t n -> p n t"), func=ACT.Tanh)
             return th
 
-        def gain(on_gpsimd, prod, units, th):
+        def gain(on_gpsimd, prod, units, th, split):
             eng, gains = (nc.gpsimd, g_col[:]) if on_gpsimd else (nc.vector, cols_ps[:, 8:24])
             c0 = 0 if weight_of[prod] == 0 else 4
             if on_gpsimd:
                 scaled = work.tile([P, 2, P, 4], BF16, name="scaled_g", tag="scaled_g", bufs=GP_BUFS, align_bytes=64)
             else:
                 scaled = work.tile([P, 2, P, 4], BF16, name="scaled", tag="scaled", bufs=5, align_bytes=64)
-            if units[0][0] == units[1][0]:
+            if split:
+                c0 += 8 * units[0][0]
+                for u in range(2):
+                    eng.tensor_tensor(
+                        out=scaled[:, u, :, :],
+                        in0=th[:, u, :, :],
+                        in1=gains[:, c0 : c0 + 4].unsqueeze(1).to_broadcast([P, P, 4]),
+                        op=ALU.mult,
+                    )
+            elif units[0][0] == units[1][0]:
                 c0 += 8 * units[0][0]
                 eng.tensor_tensor(
                     out=scaled[:].rearrange("p u n t -> p (u n) t"),
@@ -279,22 +318,20 @@ def tile_kernelbehaviouralmetrictdresidual_d1p_kernel(
             else:
                 nc.vector.scalar_tensor_tensor(out=e, in0=bank[:], scalar=-1.0, in1=e, op0=ALU.add, op1=ALU.add)
 
-        r_stage()
-        bank_t = turn(x_sb, 0)
+        bank_0 = turn_one(0)
+        grouped_0 = unload_one(nc.vector.tensor_copy, bank_0)
+        quantise_one(0, grouped_0)
         permute_words(nc.vector, 0, 0)
         permute_scales(nc.vector, 0, 0)
-        grouped = unload(nc.vector.tensor_copy, bank_t)
-        bank_t = turn(x_sb, 1)
-        distance(0)
-        quantise_x(0, 0, grouped)
-        grouped = unload(nc.scalar.copy, bank_t)
+        bank_1 = turn_one(1)
+        bank_23 = turn(x_sb, 1)
+        grouped_1 = unload_one(nc.scalar.copy, bank_1)
+        quantise_one(1, grouped_1)
+        grouped_23 = unload(nc.vector.tensor_copy, bank_23)
         permute_words(nc.vector, 0, 1)
         permute_scales(nc.vector, 0, 1)
-        g_stage()
-        quantise_x(0, 1, grouped)
-        for g in range(2):
-            permute_words(nc.vector, 1, g)
-            permute_scales(nc.vector, 1, g)
+        quantise_x(0, 1, grouped_23)
+        g_stage(0)
 
         order = []
         for a, b in (("q", "p"), ("qn", "pn")):
@@ -330,6 +367,14 @@ def tile_kernelbehaviouralmetrictdresidual_d1p_kernel(
         def first_stage(step):
             if step < len(order):
                 ths.append(features(*order[step]))
+            if step == W_AT:
+                for g in range(2):
+                    permute_words(nc.vector, 1, g)
+                    permute_scales(nc.vector, 1, g)
+            if step == R_AT:
+                r_stage()
+                r_copies()
+                g_stage(1)
             for i in DIST_AT.get(step, ()):
                 distance(i)
             for n in WIDEN_AT.get(step, ()):
@@ -351,7 +396,7 @@ def tile_kernelbehaviouralmetrictdresidual_d1p_kernel(
         for step, (prod, units) in enumerate(order):
             first_stage(step + LEAD)
             on_gp = step in ON_GPSIMD
-            scaled = gain(on_gp, prod, units, ths[step])
+            scaled = gain(on_gp, prod, units, ths[step], step == 0)
             for key in XQ_AT.get(step, ()):
                 quantise_x(*key, grouped_of[key])
             if step in FLUSH:

@@ -18,20 +18,20 @@ ALU = mybir.AluOpType
 ACT = mybir.ActivationFunctionType
 
 P = 128
-RATE = lambda step: RATES[step // 4]
-XQ_AT = {1: ((0, 2),), 3: ((0, 3),), 8: ((1, 0),), 10: ((1, 1),), 13: ((1, 2),), 16: ((1, 3),)}
-TURN_AT = {2: ((0, 2),), 3: ((0, 3),), 8: ((1, 0),), 10: ((1, 1),), 12: ((1, 2),), 15: ((1, 3),)}
-EVAC = lambda nc, which, c: nc.scalar.copy
+ON_SCALAR = frozenset((11, 13, 15, ))
+DIST_AT = {8: (0, 3), 7: (1,), 5: (2,), 10: (4,), 9: (5,), 11: (6,), 13: (7,)}
+WIDEN_AT = {7: (4,), 6: (5,), 5: (6,), 2: (7,)}
+HEAD_WIDEN = 4
+RATES = [2, 4, 4, 3, 2, 2, 3, 4, 2, 2, 4, 2, 3, 3, 3, 2, 3, 2, 2]
+LEAD = 1
+S_LAG = 1
+Q_LAG = 1
+TH_BUFS = 3
 WIDEN_SCALAR = ()
-W_AT = 1
-R_AT = 3
-ON_GPSIMD = frozenset()
-FLUSH = frozenset((0, 1, 2, 3, 4, 5, 6, 7, 8, 9, 10, 11, 12, 13, 14, 15, 16, 17, 18, 19, 20, 21, 22, 23, 24, 25, 26, 27, 28, 29, 30, 31, ))
-DIST_AT = {4: (0,), 6: (1,), 7: (2,), 9: (3,), 14: (4,), 16: (5,), 17: (6,), 18: (7,)}
-WIDEN_AT = {3: (0, 1), 5: (2, 3), 9: (4, 5), 10: (6, 7)}
-RATES = [1, 1, 1, 1, 2, 2, 2, 2]
-LEAD = 2
-GP_BUFS = 2
+W_AT = 0
+R_AT = 0
+XQ_AT = {0: ((0, 1), ), 2: ((0, 2), ), 4: ((0, 3), ), 6: ((1, 0), ), 7: ((1, 1), (1, 2), ), 10: ((1, 3), )}
+TURN_AT = {0: ((0, 1), ), 3: ((0, 2), ), 4: ((0, 3), ), 6: ((1, 0), ), 7: ((1, 1), (1, 2), ), 10: ((1, 3), )}
 
 
 def tile_kernelbehaviouralmetrictdresidual_d1p_kernel(
@@ -66,10 +66,9 @@ def tile_kernelbehaviouralmetrictdresidual_d1p_kernel(
         rows_r = keep.tile([P, 256], BF16, name="rows_r")
         rows_g = [keep.tile([P, 256], BF16, name="rows_g%d" % i) for i in range(2)]
         r_col = keep.tile([P, 8], F32, name="r_col")
-        g_col = keep.tile([P, 16], F32, name="g_col")
+        g_col = [keep.tile([P, 8], F32, name="g_col%d" % i) for i in range(2)]
         r_row = keep.tile([P, B], BF16, name="r_row")
         warm = keep.tile([P, 1], F32, name="warm")
-        cols_ps = psum.tile([P, 24], F32, name="cols_ps", tag="cols", bufs=1)
 
         x_v = x.rearrange("(n p) k -> p n k", p=P)
 
@@ -91,22 +90,24 @@ def tile_kernelbehaviouralmetrictdresidual_d1p_kernel(
         nc.vector.memset(warm[:], 0.0)
         make_identity(nc, ident_f[:])
 
-        nc.sync.dma_start(out=x_sb[:, 0, :], in_=x_v[:, 0, :])
+        xb_v = xn_bytes.rearrange("(n p) k -> p n k", p=P)
+        nc.sync.dma_start(out=x_sb[:, 0:2, :], in_=x_v[:, 0:2, :])
         load_words(0, wt_words)
         load_scales(nc.scalar, 0, wt_scales)
-        nc.sync.dma_start(out=x_sb[:, 1:4, :], in_=x_v[:, 1:4, :])
-        nc.sync.dma_start(out=x_sb[:, 4:8, :], in_=x_v[:, 4:8, :])
-        for src, dst in ((g2, rows_g[0]), (g1, rows_g[1])):
-            nc.gpsimd.dma_start(
-                out=dst[0:4, :].rearrange("t (m b) -> t m b", b=8), in_=src.rearrange("(m t b) -> t m b", t=4, b=8)
-            )
-        nc.gpsimd.dma_start(out=rows_r[0:4, :], in_=r.rearrange("(q n) -> q n", q=4))
+        nc.sync.dma_start(out=xs_sb[:], in_=xn_scale.rearrange("(n p) j -> p n j", p=P))
+        nc.sync.dma_start(out=xb_sb[:, 0:4, :], in_=xb_v[:, 0:4, :])
+        for src, dst in ((g2, rows_g[0]), (r, rows_r), (g1, rows_g[1])):
+            if dst is rows_r:
+                nc.gpsimd.dma_start(out=dst[0:4, :], in_=src.rearrange("(q n) -> q n", q=4))
+            else:
+                nc.gpsimd.dma_start(
+                    out=dst[0:4, :].rearrange("t (m b) -> t m b", b=8), in_=src.rearrange("(m t b) -> t m b", t=4, b=8)
+                )
+        nc.sync.dma_start(out=x_sb[:, 2:4, :], in_=x_v[:, 2:4, :])
         load_words(1, w_words)
         load_scales(nc.sync, 1, w_scales)
-        nc.sync.dma_start(out=xs_sb[:], in_=xn_scale.rearrange("(n p) j -> p n j", p=P))
-        xb_v = xn_bytes.rearrange("(n p) k -> p n k", p=P)
-        for half in range(2):
-            nc.sync.dma_start(out=xb_sb[:, 4 * half : 4 * half + 4, :], in_=xb_v[:, 4 * half : 4 * half + 4, :])
+        nc.sync.dma_start(out=x_sb[:, 4:8, :], in_=x_v[:, 4:8, :])
+        nc.sync.dma_start(out=xb_sb[:, 4:8, :], in_=xb_v[:, 4:8, :])
 
         nc.scalar.activation(out=warm[:], in_=warm[:], func=ACT.Tanh)
 
@@ -125,15 +126,15 @@ def tile_kernelbehaviouralmetrictdresidual_d1p_kernel(
                 in_=raw_s[i][:].bitcast(I32)[:, 128 * g : 128 * g + 128].rearrange("p (a t b) -> p t a b", t=4, b=2),
             )
 
-        r_banks = []
-
         def r_stage():
+            cols = psum.tile([P, 8], F32, name="bank_c", tag="kk", bufs=5)
             for h in range(2):
                 nc.tensor.matmul(
-                    out=cols_ps[:, 4 * h : 4 * h + 4], lhsT=rows_r[:, P * h : P * h + P], rhs=ident_b[:, 0:4], start=True, stop=True
+                    out=cols[:, 4 * h : 4 * h + 4], lhsT=rows_r[:, P * h : P * h + P], rhs=ident_b[:, 0:4], start=True, stop=True
                 )
+            nc.scalar.copy(out=r_col[:], in_=cols[:])
             for jh in range(2):
-                bank = psum.tile([P, 512], F32, name="bank_r", tag="kk", bufs=4)
+                bank = psum.tile([P, 512], F32, name="bank_r", tag="kk", bufs=5)
                 for q in range(2):
                     nc.tensor.matmul(
                         out=bank[:, 256 * q : 256 * q + 256],
@@ -142,31 +143,26 @@ def tile_kernelbehaviouralmetrictdresidual_d1p_kernel(
                         start=True,
                         stop=True,
                     )
-                r_banks.append(bank)
-
-        def r_copies():
-            for jh in range(2):
-                nc.scalar.copy(out=r_row[:, 512 * jh : 512 * jh + 512], in_=r_banks[jh][:])
-            nc.scalar.copy(out=r_col[:], in_=cols_ps[:, 0:8])
+                nc.scalar.copy(out=r_row[:, 512 * jh : 512 * jh + 512], in_=bank[:])
 
         def g_stage(side):
+            cols = psum.tile([P, 8], F32, name="bank_c", tag="kk", bufs=5)
             for h in range(2):
                 nc.tensor.matmul(
-                    out=cols_ps[:, 8 + 8 * h + 4 * side : 12 + 8 * h + 4 * side],
+                    out=cols[:, 4 * h : 4 * h + 4],
                     lhsT=rows_g[side][:, P * h : P * h + P],
                     rhs=(sel_g, ident_b)[side][:, 0:4],
                     start=True,
                     stop=True,
                 )
-            if ON_GPSIMD and side == 1:
-                nc.vector.tensor_copy(out=g_col[:], in_=cols_ps[:, 8:24])
+            nc.scalar.copy(out=g_col[side][:], in_=cols[:])
 
         def distance(i):
             c = 4 * (i % 2) + i // 2
             nc.scalar.activation(out=e_sb[:, i, :], in_=r_row[:], func=ACT.Abs, bias=r_col[:, c : c + 1], scale=-1.0)
 
         def turn(src, c):
-            bank = psum.tile([P, 2, 2, P], F32, name="bank_t", tag="kk", bufs=4)
+            bank = psum.tile([P, 2, 2, P], F32, name="bank_t", tag="kk", bufs=5)
             for a in range(2):
                 words = src[:, 2 * c + a, :].bitcast(F32)
                 for u in range(2):
@@ -224,8 +220,10 @@ def tile_kernelbehaviouralmetrictdresidual_d1p_kernel(
         weight_of = {"q": 0, "qn": 0, "p": 1, "pn": 1}
         x_of = {"q": 0, "p": 0, "qn": 1, "pn": 1}
 
-        def features(prod, units):
-            th = work.tile([P, 2, P, 4], F32, name="th", tag="th", bufs=8)
+        def features(job, prod, units):
+            by_plane = job in ON_SCALAR
+            n = len(units)
+            th = work.tile([P, n, 4, P] if by_plane else [P, n, P, 4], F32, name="th", tag="th", bufs=TH_BUFS)
             wi, xi = weight_of[prod], x_of[prod]
             for u, (g, c) in enumerate(units):
                 bank = psum.tile([P, 4, P], F32, name="bank_f", tag="mm", bufs=3)
@@ -241,58 +239,56 @@ def tile_kernelbehaviouralmetrictdresidual_d1p_kernel(
                         start=True,
                         stop=True,
                     )
-                nc.scalar.activation(out=th[:, u, :, :], in_=bank[:].rearrange("p t n -> p n t"), func=ACT.Tanh)
+                src = bank[:] if by_plane else bank[:].rearrange("p t n -> p n t")
+                nc.scalar.activation(out=th[:, u, :, :], in_=src, func=ACT.Tanh)
             return th
 
-        def gain(on_gpsimd, prod, units, th, split):
-            eng, gains = (nc.gpsimd, g_col[:]) if on_gpsimd else (nc.vector, cols_ps[:, 8:24])
-            c0 = 0 if weight_of[prod] == 0 else 4
-            if on_gpsimd:
-                scaled = work.tile([P, 2, P, 4], BF16, name="scaled_g", tag="scaled_g", bufs=GP_BUFS, align_bytes=64)
-            else:
-                scaled = work.tile([P, 2, P, 4], BF16, name="scaled", tag="scaled", bufs=5, align_bytes=64)
-            if split:
-                c0 += 8 * units[0][0]
-                for u in range(2):
-                    eng.tensor_tensor(
-                        out=scaled[:, u, :, :],
-                        in0=th[:, u, :, :],
-                        in1=gains[:, c0 : c0 + 4].unsqueeze(1).to_broadcast([P, P, 4]),
-                        op=ALU.mult,
+        def runs(units):
+            first = [u for u in range(len(units)) if units[u][0] == units[0][0]]
+            second = [u for u in range(len(units)) if u not in first]
+            return [r for r in (first, second) if r]
+
+        def gain(job, prod, units, th):
+            gains = g_col[weight_of[prod]]
+            n = len(units)
+            scaled = work.tile([P, n, P, 4], BF16, name="scaled", tag="scaled", bufs=4, align_bytes=64)
+            pieces = [[0], [1]] if job == 0 else runs(units)
+            if job in ON_SCALAR:
+                planes = work.tile([P, 4, n, P], BF16, name="planes", tag="planes", bufs=2)
+                for t in range(4):
+                    c0 = 4 * units[0][0] + t
+                    nc.vector.tensor_scalar(
+                        out=planes[:, t, :, :], in0=th[:, :, t, :], scalar1=gains[:, c0 : c0 + 1], scalar2=None, op0=ALU.mult
                     )
-            elif units[0][0] == units[1][0]:
-                c0 += 8 * units[0][0]
-                eng.tensor_tensor(
-                    out=scaled[:].rearrange("p u n t -> p (u n) t"),
-                    in0=th[:].rearrange("p u n t -> p (u n) t"),
-                    in1=gains[:, c0 : c0 + 4].unsqueeze(1).to_broadcast([P, 256, 4]),
-                    op=ALU.mult,
+                nc.scalar.copy(
+                    out=scaled[:].rearrange("p u (c i) t -> p (u c) t i", i=4),
+                    in_=planes[:].rearrange("p t u (c i) -> p (u c) t i", i=4),
                 )
-            else:
-                eng.tensor_tensor(
-                    out=scaled[:],
-                    in0=th[:],
-                    in1=gains.rearrange("p (g c) -> p g c", g=2)[:, :, c0 : c0 + 4].unsqueeze(2).to_broadcast([P, 2, P, 4]),
+                return scaled
+            for us in pieces:
+                c0 = 4 * units[us[0]][0]
+                rows = slice(us[0], us[-1] + 1)
+                nc.vector.tensor_tensor(
+                    out=scaled[:, rows, :, :].rearrange("p u n t -> p (u n) t"),
+                    in0=th[:, rows, :, :].rearrange("p u n t -> p (u n) t"),
+                    in1=gains[:, c0 : c0 + 4].unsqueeze(1).to_broadcast([P, P * len(us), 4]),
                     op=ALU.mult,
                 )
             return scaled
 
         def quantise_f(prod, units, scaled):
-            if units[0][0] == units[1][0]:
-                runs = [(units[0], 256, scaled[:])]
-            else:
-                runs = [(units[u], P, scaled[:, u : u + 1, :, :]) for u in range(2)]
-            for (g, c), width, src in runs:
-                cols = slice(P * c, P * c + width)
+            for us in runs(units):
+                g, c = units[us[0]]
+                cols = slice(P * c, P * c + P * len(us))
                 nc.vector.quantize_mx(
                     out=f_codes[prod][:, g, cols].bitcast(FP8X4),
                     scales=f_scales[prod][:, g, cols],
-                    in_=src.rearrange("p u n t -> p (u n t)"),
+                    in_=scaled[:, us[0] : us[-1] + 1, :, :].rearrange("p u n t -> p (u n t)"),
                 )
 
         def pair(i, jh, nxt):
             a, b = ("pn", "qn") if nxt else ("p", "q")
-            bank = psum.tile([P, 512], F32, name="bank_k", tag="kk", bufs=4)
+            bank = psum.tile([P, 512], F32, name="bank_k", tag="kk", bufs=5)
             rows = slice(P * i, P * i + P)
             cols = slice(512 * jh, 512 * jh + 512)
             for g in range(2):
@@ -319,27 +315,26 @@ def tile_kernelbehaviouralmetrictdresidual_d1p_kernel(
                 nc.vector.scalar_tensor_tensor(out=e, in0=bank[:], scalar=-1.0, in1=e, op0=ALU.add, op1=ALU.add)
 
         bank_0 = turn_one(0)
-        grouped_0 = unload_one(nc.vector.tensor_copy, bank_0)
-        quantise_one(0, grouped_0)
-        permute_words(nc.vector, 0, 0)
-        permute_scales(nc.vector, 0, 0)
         bank_1 = turn_one(1)
-        bank_23 = turn(x_sb, 1)
+        grouped_0 = unload_one(nc.vector.tensor_copy, bank_0)
         grouped_1 = unload_one(nc.scalar.copy, bank_1)
+        permute_words(nc.vector, 0, 0)
+        quantise_one(0, grouped_0)
+        permute_scales(nc.vector, 0, 0)
         quantise_one(1, grouped_1)
-        grouped_23 = unload(nc.vector.tensor_copy, bank_23)
+        g_stage(0)
+        for n in range(HEAD_WIDEN):
+            widen(n, False)
         permute_words(nc.vector, 0, 1)
         permute_scales(nc.vector, 0, 1)
-        quantise_x(0, 1, grouped_23)
-        g_stage(0)
 
-        order = []
-        for a, b in (("q", "p"), ("qn", "pn")):
-            for prod, c in ((a, 0), (a, 1), (b, 0), (b, 1), (a, 2), (a, 3), (b, 2), (b, 3)):
-                if prod == "pn" and c == 3:
-                    order.extend([(prod, ((0, 6), (1, 6))), (prod, ((0, 7), (1, 7)))])
-                else:
-                    order.extend([(prod, ((g, 2 * c), (g, 2 * c + 1))) for g in range(2)])
+        h0, h1 = (0, 1, 2, 3), (4, 5, 6, 7)
+        jobs = []
+        for prod, chunks in (("q", (0, 1)), ("q", (2, 3)), ("p", h0), ("q", h1), ("p", h1), ("qn", h0), ("pn", h0), ("qn", h1)):
+            for g in range(2):
+                jobs.append((prod, tuple([(g, c) for c in chunks])))
+        for chunks in ((4, 5), (6,), (7,)):
+            jobs.append(("pn", tuple([(g, c) for g in range(2) for c in chunks])))
 
         have = set()
         waiting = []
@@ -364,50 +359,48 @@ def tile_kernelbehaviouralmetrictdresidual_d1p_kernel(
         ths = []
         grouped_of = {}
 
-        def first_stage(step):
-            if step < len(order):
-                ths.append(features(*order[step]))
-            if step == W_AT:
+        def first_stage(job):
+            if job == W_AT:
                 for g in range(2):
                     permute_words(nc.vector, 1, g)
                     permute_scales(nc.vector, 1, g)
-            if step == R_AT:
-                r_stage()
-                r_copies()
+            if job < len(jobs):
+                ths.append(features(job, *jobs[job]))
+            if job == R_AT:
                 g_stage(1)
-            for i in DIST_AT.get(step, ()):
+                r_stage()
+            for i in DIST_AT.get(job, ()):
                 distance(i)
-            for n in WIDEN_AT.get(step, ()):
+            for n in WIDEN_AT.get(job, ()):
                 widen(n, n in WIDEN_SCALAR)
-            for which, c in TURN_AT.get(step, ()):
+            for which, c in TURN_AT.get(job, ()):
                 bank = turn((x_sb, xw_sb)[which], c)
-                grouped_of[(which, c)] = unload(EVAC(nc, which, c), bank)
+                grouped_of[(which, c)] = unload(nc.scalar.copy, bank)
 
-        def flush():
-            for flag in (False, True):
-                for item in due:
-                    if item[0] == flag:
-                        quantise_f(*item[1:])
-                        have.update([(item[1], g, c) for g, c in item[2]])
-            due.clear()
+        def flush(job):
+            for item in [item for item in due if item[0] <= job]:
+                due.remove(item)
+                quantise_f(*item[1:])
+                have.update([(item[1], g, c) for g, c in item[2]])
 
-        for step in range(LEAD):
-            first_stage(step)
-        for step, (prod, units) in enumerate(order):
-            first_stage(step + LEAD)
-            on_gp = step in ON_GPSIMD
-            scaled = gain(on_gp, prod, units, ths[step], step == 0)
-            for key in XQ_AT.get(step, ()):
+        for job in range(LEAD):
+            first_stage(job)
+        for job, (prod, units) in enumerate(jobs):
+            first_stage(job + LEAD)
+            scaled = gain(job, prod, units, ths[job])
+            for key in XQ_AT.get(job, ()):
                 quantise_x(*key, grouped_of[key])
-            if step in FLUSH:
-                flush()
-            due.append((on_gp, prod, units, scaled))
-            for key, bank in banks:
+            for key, bank in banks[:1]:
                 finish(*key, bank)
-            rate = RATE(step)
-            banks = [(key, pair(*key)) for key in ready[:rate]]
-            ready = ready[rate:] + ready_tiles()
-        flush()
+            flush(job)
+            due.append((job + (S_LAG if job in ON_SCALAR else Q_LAG), prod, units, scaled))
+            if Q_LAG == 0:
+                flush(job)
+            for key, bank in banks[1:]:
+                finish(*key, bank)
+            banks = [(key, pair(*key)) for key in ready[: RATES[job]]]
+            ready = ready[RATES[job] :] + ready_tiles()
+        flush(99)
         for key, bank in banks:
             finish(*key, bank)
         for key in ready + ready_tiles():

from contextlib import ExitStack

import concourse.mybir as mybir
from concourse.masks import make_identity

B, D, K = 1024, 512, 1024
FLOPS = 4 * 2 * B * D * K + 2 * 2 * B * B * K

F32 = mybir.dt.float32
BF16 = mybir.dt.bfloat16
I32 = mybir.dt.int32
U32 = mybir.dt.uint32
U8 = mybir.dt.uint8
F8 = mybir.dt.float8_e4m3fn
FP8X4 = mybir.dt.float8_e4m3fn_x4
FP4X4 = mybir.dt.float4_e2m1fn_x4
ALU = mybir.AluOpType
ACT = mybir.ActivationFunctionType

P = 128
ON_SCALAR = frozenset((11, 13, 15, ))
DIST_AT = {8: (0, 3), 7: (1,), 5: (2,), 10: (4,), 9: (5,), 11: (6,), 13: (7,)}
WIDEN_AT = {7: (4,), 6: (5,), 5: (6,), 2: (7,)}
HEAD_WIDEN = 4
RATES = [2, 4, 4, 3, 2, 2, 3, 4, 2, 2, 4, 2, 3, 3, 3, 2, 3, 2, 2]
LEAD = 1
S_LAG = 1
Q_LAG = 1
TH_BUFS = 3
WIDEN_SCALAR = ()
W_AT = 0
R_AT = 0
XQ_AT = {0: ((0, 1), ), 2: ((0, 2), ), 4: ((0, 3), ), 6: ((1, 0), ), 7: ((1, 1), (1, 2), ), 10: ((1, 3), )}
TURN_AT = {0: ((0, 1), ), 3: ((0, 2), ), 4: ((0, 3), ), 6: ((1, 0), ), 7: ((1, 1), (1, 2), ), 10: ((1, 3), )}


def tile_kernelbehaviouralmetrictdresidual_d1p_kernel(
    tc, x, xn_bytes, xn_scale, w_words, w_scales, wt_words, wt_scales, g1, g2, r, out
):
    nc = tc.nc
    with ExitStack() as ctx:
        ctx.enter_context(tc.manual_schedule())
        keep = ctx.enter_context(tc.tile_pool(name="keep", bufs=1))
        work = ctx.enter_context(tc.tile_pool(name="work", bufs=4))
        psum = ctx.enter_context(tc.psum_pool(name="psum", bufs=1))

        x_sb = keep.tile([P, 8, D], BF16, name="x_sb")
        xb_sb = keep.tile([P, 8, D], U8, name="xb_sb")
        xs_sb = keep.tile([P, 8, 4], F32, name="xs_sb")
        xw_sb = keep.tile([P, 8, D], BF16, name="xw_sb")
        x_codes = [keep.tile([P, B], U32, name="x_codes%d" % i, align_bytes=64) for i in range(2)]
        x_scales = [keep.tile([P, B], U8, name="x_scales%d" % i, align_bytes=64) for i in range(2)]
        raw_w = [keep.tile([P, 2 * K], U8, name="raw_w%d" % i, align_bytes=64) for i in range(2)]
        raw_s = [keep.tile([P, K], U8, name="raw_s%d" % i, align_bytes=64) for i in range(2)]
        perm_w = [keep.tile([P, 2 * K], U8, name="perm_w%d" % i, align_bytes=64) for i in range(2)]
        perm_s = [keep.tile([P, K], U8, name="perm_s%d" % i, align_bytes=64) for i in range(2)]
        f_codes = {}
        f_scales = {}
        for prod in ("q", "p", "qn", "pn"):
            f_codes[prod] = keep.tile([P, 2, B], U32, name="codes_%s" % prod, align_bytes=64)
            f_scales[prod] = keep.tile([P, 2, B], U8, name="scales_%s" % prod, align_bytes=64)
        e_sb = keep.tile([P, 8, B], F32, name="e_sb")
        ident_f = keep.tile([P, P], F32, name="ident_f")
        ident_b = keep.tile([P, P], BF16, name="ident_b")
        sel_g = keep.tile([P, 4], BF16, name="sel_g")
        rows_r = keep.tile([P, 256], BF16, name="rows_r")
        rows_g = [keep.tile([P, 256], BF16, name="rows_g%d" % i) for i in range(2)]
        r_col = keep.tile([P, 8], F32, name="r_col")
        g_col = [keep.tile([P, 8], F32, name="g_col%d" % i) for i in range(2)]
        r_row = keep.tile([P, B], BF16, name="r_row")
        warm = keep.tile([P, 1], F32, name="warm")

        x_v = x.rearrange("(n p) k -> p n k", p=P)

        def load_words(i, src):
            nc.sync.dma_start(out=raw_w[i][:].bitcast(I32), in_=src[0].bitcast(I32))

        def load_scales(eng, i, src):
            for quad in range(4):
                eng.dma_start(
                    out=raw_s[i][32 * quad : 32 * quad + 4, :].bitcast(I32),
                    in_=src[0, 4 * quad : 4 * quad + 4, :].bitcast(I32),
                )

        nc.vector.memset(raw_s[0][:].bitcast(I32), 0)
        nc.vector.memset(rows_r[:], 0.0)
        nc.vector.memset(rows_g[0][:], 0.0)
        nc.vector.memset(rows_g[1][:], 0.0)
        nc.vector.memset(raw_s[1][:].bitcast(I32), 0)
        nc.vector.memset(warm[:], 0.0)
        make_identity(nc, ident_f[:])

        xb_v = xn_bytes.rearrange("(n p) k -> p n k", p=P)
        nc.sync.dma_start(out=x_sb[:, 0:2, :], in_=x_v[:, 0:2, :])
        load_words(0, wt_words)
        load_scales(nc.scalar, 0, wt_scales)
        nc.sync.dma_start(out=xs_sb[:], in_=xn_scale.rearrange("(n p) j -> p n j", p=P))
        nc.sync.dma_start(out=xb_sb[:, 0:4, :], in_=xb_v[:, 0:4, :])
        for src, dst in ((g2, rows_g[0]), (r, rows_r), (g1, rows_g[1])):
            if dst is rows_r:
                nc.gpsimd.dma_start(out=dst[0:4, :], in_=src.rearrange("(q n) -> q n", q=4))
            else:
                nc.gpsimd.dma_start(
                    out=dst[0:4, :].rearrange("t (m b) -> t m b", b=8), in_=src.rearrange("(m t b) -> t m b", t=4, b=8)
                )
        nc.sync.dma_start(out=x_sb[:, 2:4, :], in_=x_v[:, 2:4, :])
        load_words(1, w_words)
        load_scales(nc.sync, 1, w_scales)
        nc.sync.dma_start(out=x_sb[:, 4:8, :], in_=x_v[:, 4:8, :])
        nc.sync.dma_start(out=xb_sb[:, 4:8, :], in_=xb_v[:, 4:8, :])

        nc.scalar.activation(out=warm[:], in_=warm[:], func=ACT.Tanh)

        nc.vector.tensor_copy(out=ident_b[:], in_=ident_f[:])
        nc.vector.tensor_scalar(out=sel_g[:], in0=ident_f[:, 0:4], scalar1=1.0 / 32.0, scalar2=None, op0=ALU.mult)

        def permute_words(eng, i, g):
            eng.tensor_copy(
                out=perm_w[i][:].bitcast(I32)[:, 256 * g : 256 * g + 256].rearrange("p (t a b) -> p t a b", t=4, b=4),
                in_=raw_w[i][:].bitcast(I32)[:, 256 * g : 256 * g + 256].rearrange("p (a t b) -> p t a b", t=4, b=4),
            )

        def permute_scales(eng, i, g):
            eng.tensor_copy(
                out=perm_s[i][:].bitcast(I32)[:, 128 * g : 128 * g + 128].rearrange("p (t a b) -> p t a b", t=4, b=2),
                in_=raw_s[i][:].bitcast(I32)[:, 128 * g : 128 * g + 128].rearrange("p (a t b) -> p t a b", t=4, b=2),
            )

        def r_stage():
            cols = psum.tile([P, 8], F32, name="bank_c", tag="kk", bufs=5)
            for h in range(2):
                nc.tensor.matmul(
                    out=cols[:, 4 * h : 4 * h + 4], lhsT=rows_r[:, P * h : P * h + P], rhs=ident_b[:, 0:4], start=True, stop=True
                )
            nc.scalar.copy(out=r_col[:], in_=cols[:])
            for jh in range(2):
                bank = psum.tile([P, 512], F32, name="bank_r", tag="kk", bufs=5)
                for q in range(2):
                    nc.tensor.matmul(
                        out=bank[:, 256 * q : 256 * q + 256],
                        lhsT=ident_b[:, 2 * jh + q : 2 * jh + q + 1].to_broadcast([P, P]),
                        rhs=rows_r[:, :],
                        start=True,
                        stop=True,
                    )
                nc.scalar.copy(out=r_row[:, 512 * jh : 512 * jh + 512], in_=bank[:])

        def g_stage(side):
            cols = psum.tile([P, 8], F32, name="bank_c", tag="kk", bufs=5)
            for h in range(2):
                nc.tensor.matmul(
                    out=cols[:, 4 * h : 4 * h + 4],
                    lhsT=rows_g[side][:, P * h : P * h + P],
                    rhs=(sel_g, ident_b)[side][:, 0:4],
                    start=True,
                    stop=True,
                )
            nc.scalar.copy(out=g_col[side][:], in_=cols[:])

        def distance(i):
            c = 4 * (i % 2) + i // 2
            nc.scalar.activation(out=e_sb[:, i, :], in_=r_row[:], func=ACT.Abs, bias=r_col[:, c : c + 1], scale=-1.0)

        def turn(src, c):
            bank = psum.tile([P, 2, 2, P], F32, name="bank_t", tag="kk", bufs=5)
            for a in range(2):
                words = src[:, 2 * c + a, :].bitcast(F32)
                for u in range(2):
                    nc.tensor.transpose(bank[:, a, u, :], words[:, u:256:2], ident_f[:])
            return bank

        def unload(eng_copy, bank):
            grouped = work.tile([P, 256, 4], BF16, name="grouped", tag="grouped", bufs=3, align_bytes=64)
            eng_copy(
                out=grouped[:].rearrange("p n t -> p (n t)").bitcast(F32).rearrange("p (a n u) -> p a n u", a=2, u=2),
                in_=bank[:].rearrange("p a u n -> p a n u"),
            )
            return grouped

        def turn_one(n):
            bank = psum.tile([P, 2, P], F32, name="bank_t1", tag="mm", bufs=3)
            words = x_sb[:, n, :].bitcast(F32)
            for u in range(2):
                nc.tensor.transpose(bank[:, u, :], words[:, u:256:2], ident_f[:])
            return bank

        def unload_one(eng_copy, bank):
            grouped = work.tile([P, P, 4], BF16, name="grouped1", tag="grouped1", bufs=2, align_bytes=64)
            eng_copy(
                out=grouped[:].rearrange("p n t -> p (n t)").bitcast(F32).rearrange("p (n u) -> p n u", u=2),
                in_=bank[:].rearrange("p u n -> p n u"),
            )
            return grouped

        def quantise_one(n, grouped):
            cols = slice(P * n, P * n + P)
            nc.vector.quantize_mx(
                out=x_codes[0][:, cols].bitcast(FP8X4),
                scales=x_scales[0][:, cols],
                in_=grouped[:].rearrange("p n t -> p (n t)"),
            )

        def quantise_x(which, c, grouped):
            cols = slice(256 * c, 256 * c + 256)
            nc.vector.quantize_mx(
                out=x_codes[which][:, cols].bitcast(FP8X4),
                scales=x_scales[which][:, cols],
                in_=grouped[:].rearrange("p n t -> p (n t)"),
            )

        def widen(n, on_scalar):
            for j in range(4):
                src = xb_sb[:, n, P * j : P * j + P].bitcast(F8)
                dst = xw_sb[:, n, P * j : P * j + P]
                if on_scalar:
                    nc.scalar.activation(out=dst, in_=src, func=ACT.Copy, scale=xs_sb[:, n, j : j + 1])
                else:
                    nc.vector.tensor_scalar(out=dst, in0=src, scalar1=xs_sb[:, n, j : j + 1], scalar2=None, op0=ALU.mult)

        weight_of = {"q": 0, "qn": 0, "p": 1, "pn": 1}
        x_of = {"q": 0, "p": 0, "qn": 1, "pn": 1}

        def features(job, prod, units):
            by_plane = job in ON_SCALAR
            n = len(units)
            th = work.tile([P, n, 4, P] if by_plane else [P, n, P, 4], F32, name="th", tag="th", bufs=TH_BUFS)
            wi, xi = weight_of[prod], x_of[prod]
            for u, (g, c) in enumerate(units):
                bank = psum.tile([P, 4, P], F32, name="bank_f", tag="mm", bufs=3)
                toks = slice(P * c, P * c + P)
                for t in range(4):
                    s = 4 * g + t
                    nc.tensor.matmul_mx(
                        out=bank[:, t, :],
                        lhsT=perm_w[wi][:, 256 * s : 256 * s + 256].bitcast(FP4X4),
                        lhsT_scale=perm_s[wi][:, P * s : P * s + P],
                        rhs=x_codes[xi][:, toks].bitcast(FP8X4),
                        rhs_scale=x_scales[xi][:, toks],
                        start=True,
                        stop=True,
                    )
                src = bank[:] if by_plane else bank[:].rearrange("p t n -> p n t")
                nc.scalar.activation(out=th[:, u, :, :], in_=src, func=ACT.Tanh)
            return th

        def runs(units):
            first = [u for u in range(len(units)) if units[u][0] == units[0][0]]
            second = [u for u in range(len(units)) if u not in first]
            return [r for r in (first, second) if r]

        def gain(job, prod, units, th):
            gains = g_col[weight_of[prod]]
            n = len(units)
            scaled = work.tile([P, n, P, 4], BF16, name="scaled", tag="scaled", bufs=4, align_bytes=64)
            pieces = [[0], [1]] if job == 0 else runs(units)
            if job in ON_SCALAR:
                planes = work.tile([P, 4, n, P], BF16, name="planes", tag="planes", bufs=2)
                for t in range(4):
                    c0 = 4 * units[0][0] + t
                    nc.vector.tensor_scalar(
                        out=planes[:, t, :, :], in0=th[:, :, t, :], scalar1=gains[:, c0 : c0 + 1], scalar2=None, op0=ALU.mult
                    )
                nc.scalar.copy(
                    out=scaled[:].rearrange("p u (c i) t -> p (u c) t i", i=4),
                    in_=planes[:].rearrange("p t u (c i) -> p (u c) t i", i=4),
                )
                return scaled
            for us in pieces:
                c0 = 4 * units[us[0]][0]
                rows = slice(us[0], us[-1] + 1)
                nc.vector.tensor_tensor(
                    out=scaled[:, rows, :, :].rearrange("p u n t -> p (u n) t"),
                    in0=th[:, rows, :, :].rearrange("p u n t -> p (u n) t"),
                    in1=gains[:, c0 : c0 + 4].unsqueeze(1).to_broadcast([P, P * len(us), 4]),
                    op=ALU.mult,
                )
            return scaled

        def quantise_f(prod, units, scaled):
            for us in runs(units):
                g, c = units[us[0]]
                cols = slice(P * c, P * c + P * len(us))
                nc.vector.quantize_mx(
                    out=f_codes[prod][:, g, cols].bitcast(FP8X4),
                    scales=f_scales[prod][:, g, cols],
                    in_=scaled[:, us[0] : us[-1] + 1, :, :].rearrange("p u n t -> p (u n t)"),
                )

        def pair(i, jh, nxt):
            a, b = ("pn", "qn") if nxt else ("p", "q")
            bank = psum.tile([P, 512], F32, name="bank_k", tag="kk", bufs=5)
            rows = slice(P * i, P * i + P)
            cols = slice(512 * jh, 512 * jh + 512)
            for g in range(2):
                nc.tensor.matmul_mx(
                    out=bank[:],
                    lhsT=f_codes[a][:, g, rows].bitcast(FP8X4),
                    lhsT_scale=f_scales[a][:, g, rows],
                    rhs=f_codes[b][:, g, cols].bitcast(FP8X4),
                    rhs_scale=f_scales[b][:, g, cols],
                    start=(g == 0),
                    stop=(g == 1),
                )
            return bank

        def finish(i, jh, nxt, bank):
            rows = slice(P * i, P * i + P)
            cols = slice(512 * jh, 512 * jh + 512)
            e = e_sb[:, i, cols]
            if nxt:
                res = work.tile([P, 512], F32, name="res", tag="res", bufs=6)
                nc.vector.scalar_tensor_tensor(out=res[:], in0=bank[:], scalar=-0.9, in1=e, op0=ALU.mult, op1=ALU.add)
                nc.sync.dma_start(out=out[rows, cols], in_=res[:])
            else:
                nc.vector.scalar_tensor_tensor(out=e, in0=bank[:], scalar=-1.0, in1=e, op0=ALU.add, op1=ALU.add)

        bank_0 = turn_one(0)
        bank_1 = turn_one(1)
        grouped_0 = unload_one(nc.vector.tensor_copy, bank_0)
        grouped_1 = unload_one(nc.scalar.copy, bank_1)
        permute_words(nc.vector, 0, 0)
        quantise_one(0, grouped_0)
        permute_scales(nc.vector, 0, 0)
        quantise_one(1, grouped_1)
        g_stage(0)
        for n in range(HEAD_WIDEN):
            widen(n, False)
        permute_words(nc.vector, 0, 1)
        permute_scales(nc.vector, 0, 1)

        h0, h1 = (0, 1, 2, 3), (4, 5, 6, 7)
        jobs = []
        for prod, chunks in (("q", (0, 1)), ("q", (2, 3)), ("p", h0), ("q", h1), ("p", h1), ("qn", h0), ("pn", h0), ("qn", h1)):
            for g in range(2):
                jobs.append((prod, tuple([(g, c) for c in chunks])))
        for chunks in ((4, 5), (6,), (7,)):
            jobs.append(("pn", tuple([(g, c) for g in range(2) for c in chunks])))

        have = set()
        waiting = []
        for nxt in (0, 1):
            for jh in range(2):
                waiting.extend([(i, jh, nxt) for i in range(8)])

        def ready_tiles():
            found = []
            for i, jh, nxt in waiting:
                a, b = ("pn", "qn") if nxt else ("p", "q")
                need = set([(a, g, i) for g in range(2)] + [(b, g, 4 * jh + m) for g in range(2) for m in range(4)])
                if need <= have:
                    found.append((i, jh, nxt))
            for key in found:
                waiting.remove(key)
            return found

        ready = []
        banks = []
        due = []
        ths = []
        grouped_of = {}

        def first_stage(job):
            if job == W_AT:
                for g in range(2):
                    permute_words(nc.vector, 1, g)
                    permute_scales(nc.vector, 1, g)
            if job < len(jobs):
                ths.append(features(job, *jobs[job]))
            if job == R_AT:
                g_stage(1)
                r_stage()
            for i in DIST_AT.get(job, ()):
                distance(i)
            for n in WIDEN_AT.get(job, ()):
                widen(n, n in WIDEN_SCALAR)
            for which, c in TURN_AT.get(job, ()):
                bank = turn((x_sb, xw_sb)[which], c)
                grouped_of[(which, c)] = unload(nc.scalar.copy, bank)

        def flush(job):
            for item in [item for item in due if item[0] <= job]:
                due.remove(item)
                quantise_f(*item[1:])
                have.update([(item[1], g, c) for g, c in item[2]])

        for job in range(LEAD):
            first_stage(job)
        for job, (prod, units) in enumerate(jobs):
            first_stage(job + LEAD)
            scaled = gain(job, prod, units, ths[job])
            for key in XQ_AT.get(job, ()):
                quantise_x(*key, grouped_of[key])
            for key, bank in banks[:1]:
                finish(*key, bank)
            flush(job)
            due.append((job + (S_LAG if job in ON_SCALAR else Q_LAG), prod, units, scaled))
            if Q_LAG == 0:
                flush(job)
            for key, bank in banks[1:]:
                finish(*key, bank)
            banks = [(key, pair(*key)) for key in ready[: RATES[job]]]
            ready = ready[RATES[job] :] + ready_tiles()
        flush(99)
        for key, bank in banks:
            finish(*key, bank)
        for key in ready + ready_tiles():
            finish(*key, pair(*key))
